import numpy as np
import ml_dtypes


def mxq(x, axis, fmt="e4m3"):
    dtype, down = {"e4m3": (ml_dtypes.float8_e4m3fn, 7), "e5m2": (ml_dtypes.float8_e5m2, 14)}[fmt]
    v = np.moveaxis(np.asarray(x, np.float32).astype(ml_dtypes.bfloat16).astype(np.float64), axis, -1)
    blocks = v.reshape(v.shape[:-1] + (-1, 32))
    amax = np.abs(blocks).max(-1, keepdims=True)
    byte = np.maximum(np.where(amax > 0, np.frexp(amax)[1] - 1 + 127, 0) - down, 1)
    scale = np.exp2(byte - 127.0)
    codes = (blocks / scale).astype(np.float32).astype(dtype).astype(np.float64)
    return np.moveaxis((codes * scale).reshape(v.shape), -1, axis)


WIDE = False


def mx_kscale(k):
    if not WIDE:
        return np.ones(k)
    levels = np.array([10, -10, 5, -5, 0])
    if k % 512:
        return np.exp2(np.random.permutation(np.resize(levels, k // 32))).repeat(32)
    a = np.empty((k // 512, 16))
    for p in range(k // 512):
        a[p, :8] = np.random.permutation(np.resize(levels, 8))
        for g in range(8):
            far = levels[np.abs(levels - a[p, g]) >= 10]
            a[p, g + 8] = far[np.random.randint(len(far))]
    return np.exp2(a.ravel()).repeat(32)


def f64(x):
    return np.asarray(x).astype(np.float64)


def striped(idx):
    return np.tile(np.asarray(idx).reshape(-1, 16).T, (8, 1)).astype(np.uint16)


def unstriped(offs):
    return offs[:16].T.reshape(-1).astype(np.int64)


E2M1 = np.array([0.0, 0.5, 1.0, 1.5, 2.0, 3.0, 4.0, 6.0, -0.0, -0.5, -1.0, -1.5, -2.0, -3.0, -4.0, -6.0])


def pack_weight(w, fmt):
    k, n = w.shape
    w = f64(np.asarray(w, np.float32).astype(ml_dtypes.bfloat16)).reshape(k // 32, 32, n)
    amax = np.abs(w).max(1)
    if fmt == "e4m3":
        byte = np.frexp(amax)[1] - 1 + 127 - 7
    else:
        mant, ex = np.frexp(amax / 6.0)
        byte = np.where(mant > 0.5, ex, ex - 1) + 127
    byte = np.clip(np.where(amax > 0, byte, 1), 1, 254)
    scaled = (w * np.exp2(127.0 - byte)[:, None, :]).reshape(k, n).astype(np.float32)
    by_word = np.ascontiguousarray(scaled.reshape(k // 512, 128, 4, n).transpose(0, 1, 3, 2))
    if fmt == "e4m3":
        words = by_word.astype(ml_dtypes.float8_e4m3fn).view(np.uint8)
    else:
        c = by_word.astype(ml_dtypes.float4_e2m1fn).view(np.uint8) & 0xF
        words = (c[..., 0::2] | (c[..., 1::2] << 4)).reshape(k // 512, 128, 2 * n)
    return np.ascontiguousarray(words), np.ascontiguousarray(byte.astype(np.uint8).reshape(k // 512, 16, n))


def unpack_weight(words, scales, fmt):
    g, _, n = scales.shape
    words = np.ascontiguousarray(words).reshape(g, 128, n, -1)
    if fmt == "e4m3":
        vals = words.view(ml_dtypes.float8_e4m3fn).astype(np.float64)
    else:
        nib = np.empty((g, 128, n, 4), np.uint8)
        nib[..., 0::2] = words & 0xF
        nib[..., 1::2] = words >> 4
        vals = E2M1[nib]
    vals = vals * np.repeat(np.exp2(scales.astype(np.float64) - 127.0), 8, axis=1)[..., None]
    return vals.transpose(0, 1, 3, 2).reshape(g * 512, n)


K, T, J, R, O, N, E = 512, 1024, 256, 512, 128, 256, 256


def setup_inputs():
    n = np.random.standard_normal
    idx = np.random.permutation(T)[:J]
    idx2 = np.random.permutation(J)[:O]
    idx3 = np.random.permutation(E)[:O]
    fk = mx_kscale(K)
    fr = mx_kscale(R)
    xtp = pack_weight(n((K, T)) / fk[:, None], "e2m1")
    wp = pack_weight(n((K, R)) * 1 / np.sqrt(K) * fk[:, None], "e4m3")
    wbp = pack_weight(n((R, N)) * 1 / np.sqrt(R) / fr[:, None], "e2m1")
    return {
        "xt_words": xtp[0],
        "xt_scales": xtp[1],
        "w_words": wp[0],
        "w_scales": wp[1],
        "lo": (np.random.uniform(-1.0, 1.0, (R, 1)) + np.log(fr)[:, None]).astype(np.float32),
        "wb_words": wbp[0],
        "wb_scales": wbp[1],
        "so": (np.random.uniform(0.5, 1.6, (N, 1))).astype(np.float32),
        "offs": striped(idx),
        "offs2": striped(idx2),
        "offs3": striped(idx3),
    }


def reference(xt_words, xt_scales, w_words, w_scales, lo, wb_words, wb_scales, so, offs, offs2, offs3):
    idx = unstriped(offs)
    idx2 = unstriped(offs2)
    idx3 = unstriped(offs3)
    xtu = unpack_weight(xt_words, xt_scales, "e2m1")
    wu = unpack_weight(w_words, w_scales, "e4m3")
    wbu = unpack_weight(wb_words, wb_scales, "e2m1")
    xtidxg = xtu[:, idx]
    a = wu.T @ xtidxg
    nb = f64(lo) - np.max(a, axis=1, keepdims=True)
    hid = np.exp(a[:, idx2] + nb)
    hidq = mxq(hid, 0, "e4m3")
    p = wbu.T @ hidq
    y = np.zeros((N, E))
    y[:, idx3] = p * f64(so)
    return y

@@ -1,0 +1,121 @@
+from contextlib import ExitStack
+
+import concourse.mybir as mybir
+
+K, T, J, R, O, N, E = 512, 1024, 256, 512, 128, 256, 256
+FLOPS = 2 * K * R * J + 2 * R * N * O
+
+F32 = mybir.dt.float32
+BF16 = mybir.dt.bfloat16
+I32 = mybir.dt.int32
+U32 = mybir.dt.uint32
+U16 = mybir.dt.uint16
+U8 = mybir.dt.uint8
+FP8X4 = mybir.dt.float8_e4m3fn_x4
+FP4X4 = mybir.dt.float4_e2m1fn_x4
+ALU = mybir.AluOpType
+ACT = mybir.ActivationFunctionType
+
+P = 128
+PACK = 4
+QUADS = 4
+CHUNKS = N // P
+
+
+def tile_list_peaked_kernel(tc, xt_words, xt_scales, w_words, w_scales, lo, wb_words, wb_scales, so, offs, offs2, offs3, out):
+    nc = tc.nc
+    with ExitStack() as ctx:
+        sb = ctx.enter_context(tc.tile_pool(name="sb", bufs=1))
+        ps = ctx.enter_context(tc.psum_pool(name="ps", bufs=1))
+
+        def tl(name, cols, dtype, rows=P, tag=None):
+            return sb.tile([rows, cols], dtype, name=name, tag=tag or name, align_bytes=64)
+
+        list1 = sb.tile([P, J // 16], U16, name="list1")
+        list2 = sb.tile([P, O // 16], U16, name="list2")
+        list3 = sb.tile([P, O // 16], U16, name="list3")
+        xw = tl("xw", T, U16)
+        xs = tl("xs", T, U8)
+        ww = tl("ww", R, U32)
+        ws_rows = tl("ws_rows", QUADS * R, U8, rows=4)
+        ws = tl("ws", R, U8)
+        bs = tl("bs", N, U8)
+        lo_sb = tl("lo_sb", PACK, F32)
+        so_sb = tl("so_sb", CHUNKS, F32)
+        pages = [tl(f"page{c}", E, F32) for c in range(CHUNKS)]
+
+        nc.vector.memset(xs[:].bitcast(I32), 0)
+        nc.vector.memset(ws[:].bitcast(I32), 0)
+
+        nc.sync.dma_start(
+            ws_rows[:].bitcast(I32).rearrange("r (q c) -> r q c", q=QUADS),
+            w_scales[0].bitcast(I32).rearrange("(q r) c -> r q c", q=QUADS),
+        )
+        nc.sync.dma_start(xw[:].bitcast(I32), xt_words[0].bitcast(I32))
+        nc.sync.dma_start(list1[:], offs)
+        nc.sync.dma_start(ww[:].bitcast(I32), w_words[0].rearrange("p n t -> p (n t)").bitcast(I32))
+        for q in range(QUADS):
+            nc.sync.dma_start(xs[32 * q : 32 * q + 4, :].bitcast(I32), xt_scales[0, 4 * q : 4 * q + 4, :].bitcast(I32))
+        nc.sync.dma_start(lo_sb[:], lo.rearrange("(p t) one -> p (t one)", t=PACK))
+        nc.sync.dma_start(list2[:], offs2)
+        bw = tl("bw", 2 * N, U8)
+        nc.sync.dma_start(bw[:].bitcast(I32), wb_words[0].bitcast(I32))
+        nc.vector.memset(bs[:].bitcast(I32), 0)
+        for q in range(QUADS):
+            nc.sync.dma_start(bs[32 * q : 32 * q + 4, :].bitcast(I32), wb_scales[0, 4 * q : 4 * q + 4, :].bitcast(I32))
+        nc.sync.dma_start(list3[:], offs3)
+        with nc.allow_non_contiguous_dma(reason="one weight a partition for each chunk of output features"):
+            nc.sync.dma_start(so_sb[:], so.rearrange("(c p) one -> p (c one)", p=P))
+        for c in range(CHUNKS):
+            nc.vector.memset(pages[c][:], 0.0)
+
+        ws32 = ws[:].bitcast(I32)
+        rows32 = ws_rows[:].bitcast(I32)
+        for q in range(QUADS):
+            nc.vector.tensor_copy(ws32[32 * q : 32 * q + 4, :], rows32[:, q * (R // 4) : (q + 1) * (R // 4)])
+
+        ws_first = tl("ws_first", P, U8)
+        ws_rest = tl("ws_rest", (PACK - 1) * P, U8)
+        ws_by_slot = ws[:].rearrange("p (m t) -> p t m", t=PACK)
+        nc.vector.tensor_copy(ws_first[:], ws_by_slot[:, 0, :])
+
+        gs = tl("gs", J, U8)
+        gw = tl("gw", J, U16)
+        nc.vector.tensor_copy(gw[:], xw[:].indirect(list1[:]))
+        nc.vector.tensor_copy(gs[:], xs[:].indirect(list1[:]))
+        nc.vector.tensor_copy(ws_rest[:].rearrange("p (t m) -> p t m", t=PACK - 1), ws_by_slot[:, 1:PACK, :])
+
+        ww_by_slot = ww[:].rearrange("p (m t) -> p t m", t=PACK)
+        wt = [tl(f"wt{t}", P, U32) for t in range(PACK)]
+        for t in range(PACK):
+            nc.scalar.copy(wt[t][:], ww_by_slot[:, t, :])
+
+        hid = tl("hid", PACK * O, BF16)
+        for t in range(PACK):
+            acc = ps.tile([P, J], F32, name=f"acc{t}")
+            scale_cols = ws_first[:] if t == 0 else ws_rest[:, (t - 1) * P : t * P]
+            nc.tensor.matmul_mx(
+                out=acc[:], lhsT=wt[t][:].bitcast(FP8X4), lhsT_scale=scale_cols,
+                rhs=gw[:].bitcast(FP4X4), rhs_scale=gs[:], start=True, stop=True,
+            )
+            a = tl(f"a{t}", J, F32)
+            top = tl(f"top{t}", 1, F32)
+            nb = tl(f"nb{t}", 1, F32)
+            nc.vector.tensor_scalar(out=a[:], in0=acc[:], scalar1=1.0, scalar2=None, op0=ALU.mult, op1=ALU.max, accum_out=top[:])
+            nc.vector.tensor_tensor(out=nb[:], in0=lo_sb[:, t : t + 1], in1=top[:], op=ALU.subtract)
+            nc.scalar.activation(out=hid[:, t : PACK * O : PACK], in_=a[:].indirect(list2[:]), func=ACT.Exp, bias=nb[:])
+
+        hw = tl("hw", O, U32)
+        hs = tl("hs", O, U8)
+        nc.vector.quantize_mx(out=hw[:].bitcast(FP8X4), scales=hs[:], in_=hid[:])
+
+        for c in range(CHUNKS):
+            acc2 = ps.tile([P, O], F32, name=f"pacc{c}")
+            nc.tensor.matmul_mx(
+                out=acc2[:], lhsT=bw[:, 2 * P * c : 2 * P * (c + 1)].bitcast(FP4X4), lhsT_scale=bs[:, P * c : P * (c + 1)],
+                rhs=hw[:].bitcast(FP8X4), rhs_scale=hs[:], start=True, stop=True,
+            )
+            prod = tl(f"prod{c}", O, F32)
+            nc.vector.tensor_copy(prod[:], acc2[:])
+            nc.scalar.activation(out=pages[c][:].indirect(list3[:]), in_=prod[:], func=ACT.Copy, scale=so_sb[:, c : c + 1])
+            nc.sync.dma_start(out[P * c : P * (c + 1), :], pages[c][:])

@@ -44,7 +44,8 @@ def tile_list_peaked_kernel(tc, xt_words, xt_scales, w_words, w_scales, lo, wb_w
         so_sb = tl("so_sb", CHUNKS, F32)
         pages = [tl(f"page{c}", E, F32) for c in range(CHUNKS)]
 
-        nc.vector.memset(xs[:].bitcast(I32), 0)
+        nc.vector.memset(xs[:, : T // 2].bitcast(I32), 0)
+        nc.gpsimd.memset(xs[:, T // 2 :].bitcast(I32), 0)
         nc.vector.memset(ws[:].bitcast(I32), 0)
 
         nc.sync.dma_start(
@@ -53,9 +54,10 @@ def tile_list_peaked_kernel(tc, xt_words, xt_scales, w_words, w_scales, lo, wb_w
         )
         nc.sync.dma_start(xw[:].bitcast(I32), xt_words[0].bitcast(I32))
         nc.sync.dma_start(list1[:], offs)
-        nc.sync.dma_start(ww[:].bitcast(I32), w_words[0].rearrange("p n t -> p (n t)").bitcast(I32))
         for q in range(QUADS):
-            nc.sync.dma_start(xs[32 * q : 32 * q + 4, :].bitcast(I32), xt_scales[0, 4 * q : 4 * q + 4, :].bitcast(I32))
+            eng = nc.scalar if q % 2 == 0 else nc.sync
+            eng.dma_start(xs[32 * q : 32 * q + 4, :].bitcast(I32), xt_scales[0, 4 * q : 4 * q + 4, :].bitcast(I32))
+        nc.sync.dma_start(ww[:].bitcast(I32), w_words[0].rearrange("p n t -> p (n t)").bitcast(I32))
         nc.sync.dma_start(lo_sb[:], lo.rearrange("(p t) one -> p (t one)", t=PACK))
         nc.sync.dma_start(list2[:], offs2)
         bw = tl("bw", 2 * N, U8)
@@ -74,16 +76,16 @@ def tile_list_peaked_kernel(tc, xt_words, xt_scales, w_words, w_scales, lo, wb_w
         for q in range(QUADS):
             nc.vector.tensor_copy(ws32[32 * q : 32 * q + 4, :], rows32[:, q * (R // 4) : (q + 1) * (R // 4)])
 
-        ws_first = tl("ws_first", P, U8)
-        ws_rest = tl("ws_rest", (PACK - 1) * P, U8)
+        ws_first = tl("ws_first", 2 * P, U8)
         ws_by_slot = ws[:].rearrange("p (m t) -> p t m", t=PACK)
-        nc.vector.tensor_copy(ws_first[:], ws_by_slot[:, 0, :])
+        nc.vector.tensor_copy(ws_first[:].rearrange("p (t m) -> p t m", t=2), ws_by_slot[:, 0:2, :])
 
         gs = tl("gs", J, U8)
         gw = tl("gw", J, U16)
         nc.vector.tensor_copy(gw[:], xw[:].indirect(list1[:]))
         nc.vector.tensor_copy(gs[:], xs[:].indirect(list1[:]))
-        nc.vector.tensor_copy(ws_rest[:].rearrange("p (t m) -> p t m", t=PACK - 1), ws_by_slot[:, 1:PACK, :])
+        ws_rest = tl("ws_rest", 2 * P, U8, tag="xs")
+        nc.vector.tensor_copy(ws_rest[:].rearrange("p (t m) -> p t m", t=2), ws_by_slot[:, 2:PACK, :])
 
         ww_by_slot = ww[:].rearrange("p (m t) -> p t m", t=PACK)
         wt = [tl(f"wt{t}", P, U32) for t in range(PACK)]
@@ -93,7 +95,7 @@ def tile_list_peaked_kernel(tc, xt_words, xt_scales, w_words, w_scales, lo, wb_w
         hid = tl("hid", PACK * O, BF16)
         for t in range(PACK):
             acc = ps.tile([P, J], F32, name=f"acc{t}")
-            scale_cols = ws_first[:] if t == 0 else ws_rest[:, (t - 1) * P : t * P]
+            scale_cols = (ws_first if t < 2 else ws_rest)[:, (t % 2) * P : (t % 2 + 1) * P]
             nc.tensor.matmul_mx(
                 out=acc[:], lhsT=wt[t][:].bitcast(FP8X4), lhsT_scale=scale_cols,
                 rhs=gw[:].bitcast(FP4X4), rhs_scale=gs[:], start=True, stop=True,

@@ -74,18 +74,19 @@ def tile_list_peaked_kernel(tc, xt_words, xt_scales, w_words, w_scales, lo, wb_w
         ws32 = ws[:].bitcast(I32)
         rows32 = ws_rows[:].bitcast(I32)
         for q in range(QUADS):
-            nc.vector.tensor_copy(ws32[32 * q : 32 * q + 4, :], rows32[:, q * (R // 4) : (q + 1) * (R // 4)])
+            eng = nc.gpsimd if q == 0 else nc.vector
+            eng.tensor_copy(ws32[32 * q : 32 * q + 4, :], rows32[:, q * (R // 4) : (q + 1) * (R // 4)])
 
-        ws_first = tl("ws_first", 2 * P, U8)
+        wst = [tl(f"wst{t}", P, U8) for t in range(PACK)]
         ws_by_slot = ws[:].rearrange("p (m t) -> p t m", t=PACK)
-        nc.vector.tensor_copy(ws_first[:].rearrange("p (t m) -> p t m", t=2), ws_by_slot[:, 0:2, :])
+        for t in range(PACK):
+            nc.gpsimd.tensor_copy(wst[t][:], ws_by_slot[:, t, :])
 
         gs = tl("gs", J, U8)
         gw = tl("gw", J, U16)
         nc.vector.tensor_copy(gw[:], xw[:].indirect(list1[:]))
-        nc.vector.tensor_copy(gs[:], xs[:].indirect(list1[:]))
-        ws_rest = tl("ws_rest", 2 * P, U8, tag="xs")
-        nc.vector.tensor_copy(ws_rest[:].rearrange("p (t m) -> p t m", t=2), ws_by_slot[:, 2:PACK, :])
+        for h in range(2):
+            nc.vector.tensor_copy(gs[:, h * P : (h + 1) * P], xs[:].indirect(list1[:, h * 8 : (h + 1) * 8]))
 
         ww_by_slot = ww[:].rearrange("p (m t) -> p t m", t=PACK)
         wt = [tl(f"wt{t}", P, U32) for t in range(PACK)]
@@ -95,16 +96,21 @@ def tile_list_peaked_kernel(tc, xt_words, xt_scales, w_words, w_scales, lo, wb_w
         hid = tl("hid", PACK * O, BF16)
         for t in range(PACK):
             acc = ps.tile([P, J], F32, name=f"acc{t}")
-            scale_cols = (ws_first if t < 2 else ws_rest)[:, (t % 2) * P : (t % 2 + 1) * P]
-            nc.tensor.matmul_mx(
-                out=acc[:], lhsT=wt[t][:].bitcast(FP8X4), lhsT_scale=scale_cols,
-                rhs=gw[:].bitcast(FP4X4), rhs_scale=gs[:], start=True, stop=True,
-            )
+            width = J // 2 if t == 0 else J
+            for j0 in range(0, J, width):
+                cols = slice(j0, j0 + width)
+                nc.tensor.matmul_mx(
+                    out=acc[:, cols], lhsT=wt[t][:].bitcast(FP8X4), lhsT_scale=wst[t][:],
+                    rhs=gw[:, cols].bitcast(FP4X4), rhs_scale=gs[:, cols], start=True, stop=True,
+                )
             a = tl(f"a{t}", J, F32)
             top = tl(f"top{t}", 1, F32)
             nb = tl(f"nb{t}", 1, F32)
             nc.vector.tensor_scalar(out=a[:], in0=acc[:], scalar1=1.0, scalar2=None, op0=ALU.mult, op1=ALU.max, accum_out=top[:])
-            nc.vector.tensor_tensor(out=nb[:], in0=lo_sb[:, t : t + 1], in1=top[:], op=ALU.subtract)
+            if t == 0:
+                nc.scalar.activation(out=nb[:], in_=top[:], func=ACT.Identity, bias=lo_sb[:, t : t + 1], scale=-1.0)
+            else:
+                nc.vector.tensor_tensor(out=nb[:], in0=lo_sb[:, t : t + 1], in1=top[:], op=ALU.subtract)
             nc.scalar.activation(out=hid[:, t : PACK * O : PACK], in_=a[:].indirect(list2[:]), func=ACT.Exp, bias=nb[:])
 
         hw = tl("hw", O, U32)

from contextlib import ExitStack

import concourse.mybir as mybir

K, T, J, R, O, N, E = 512, 1024, 256, 512, 128, 256, 256
FLOPS = 2 * K * R * J + 2 * R * N * O

F32 = mybir.dt.float32
BF16 = mybir.dt.bfloat16
I32 = mybir.dt.int32
U32 = mybir.dt.uint32
U16 = mybir.dt.uint16
U8 = mybir.dt.uint8
FP8X4 = mybir.dt.float8_e4m3fn_x4
FP4X4 = mybir.dt.float4_e2m1fn_x4
ALU = mybir.AluOpType
ACT = mybir.ActivationFunctionType

P = 128
PACK = 4
QUADS = 4
CHUNKS = N // P


def tile_list_peaked_kernel(tc, xt_words, xt_scales, w_words, w_scales, lo, wb_words, wb_scales, so, offs, offs2, offs3, out):
    nc = tc.nc
    with ExitStack() as ctx:
        sb = ctx.enter_context(tc.tile_pool(name="sb", bufs=1))
        ps = ctx.enter_context(tc.psum_pool(name="ps", bufs=1))

        def tl(name, cols, dtype, rows=P, tag=None):
            return sb.tile([rows, cols], dtype, name=name, tag=tag or name, align_bytes=64)

        list1 = sb.tile([P, J // 16], U16, name="list1")
        list2 = sb.tile([P, O // 16], U16, name="list2")
        list3 = sb.tile([P, O // 16], U16, name="list3")
        xw = tl("xw", T, U16)
        xs = tl("xs", T, U8)
        ww = tl("ww", R, U32)
        ws_rows = tl("ws_rows", QUADS * R, U8, rows=4)
        ws = tl("ws", R, U8)
        bs = tl("bs", N, U8)
        lo_sb = tl("lo_sb", PACK, F32)
        so_sb = tl("so_sb", CHUNKS, F32)
        pages = [tl(f"page{c}", E, F32) for c in range(CHUNKS)]

        nc.vector.memset(xs[:, : T // 2].bitcast(I32), 0)
        nc.gpsimd.memset(xs[:, T // 2 :].bitcast(I32), 0)
        nc.vector.memset(ws[:].bitcast(I32), 0)

        nc.sync.dma_start(
            ws_rows[:].bitcast(I32).rearrange("r (q c) -> r q c", q=QUADS),
            w_scales[0].bitcast(I32).rearrange("(q r) c -> r q c", q=QUADS),
        )
        nc.sync.dma_start(xw[:].bitcast(I32), xt_words[0].bitcast(I32))
        nc.sync.dma_start(list1[:], offs)
        for q in range(QUADS):
            eng = nc.scalar if q % 2 == 0 else nc.sync
            eng.dma_start(xs[32 * q : 32 * q + 4, :].bitcast(I32), xt_scales[0, 4 * q : 4 * q + 4, :].bitcast(I32))
        nc.sync.dma_start(ww[:].bitcast(I32), w_words[0].rearrange("p n t -> p (n t)").bitcast(I32))
        nc.sync.dma_start(lo_sb[:], lo.rearrange("(p t) one -> p (t one)", t=PACK))
        nc.sync.dma_start(list2[:], offs2)
        bw = tl("bw", 2 * N, U8)
        nc.sync.dma_start(bw[:].bitcast(I32), wb_words[0].bitcast(I32))
        nc.vector.memset(bs[:].bitcast(I32), 0)
        for q in range(QUADS):
            nc.sync.dma_start(bs[32 * q : 32 * q + 4, :].bitcast(I32), wb_scales[0, 4 * q : 4 * q + 4, :].bitcast(I32))
        nc.sync.dma_start(list3[:], offs3)
        with nc.allow_non_contiguous_dma(reason="one weight a partition for each chunk of output features"):
            nc.sync.dma_start(so_sb[:], so.rearrange("(c p) one -> p (c one)", p=P))
        for c in range(CHUNKS):
            nc.vector.memset(pages[c][:], 0.0)

        ws32 = ws[:].bitcast(I32)
        rows32 = ws_rows[:].bitcast(I32)
        for q in range(QUADS):
            eng = nc.gpsimd if q == 0 else nc.vector
            eng.tensor_copy(ws32[32 * q : 32 * q + 4, :], rows32[:, q * (R // 4) : (q + 1) * (R // 4)])

        wst = [tl(f"wst{t}", P, U8) for t in range(PACK)]
        ws_by_slot = ws[:].rearrange("p (m t) -> p t m", t=PACK)
        for t in range(PACK):
            nc.gpsimd.tensor_copy(wst[t][:], ws_by_slot[:, t, :])

        gs = tl("gs", J, U8)
        gw = tl("gw", J, U16)
        nc.vector.tensor_copy(gw[:], xw[:].indirect(list1[:]))
        for h in range(2):
            nc.vector.tensor_copy(gs[:, h * P : (h + 1) * P], xs[:].indirect(list1[:, h * 8 : (h + 1) * 8]))

        ww_by_slot = ww[:].rearrange("p (m t) -> p t m", t=PACK)
        wt = [tl(f"wt{t}", P, U32) for t in range(PACK)]
        for t in range(PACK):
            nc.scalar.copy(wt[t][:], ww_by_slot[:, t, :])

        hid = tl("hid", PACK * O, BF16)
        for t in range(PACK):
            acc = ps.tile([P, J], F32, name=f"acc{t}")
            width = J // 2 if t == 0 else J
            for j0 in range(0, J, width):
                cols = slice(j0, j0 + width)
                nc.tensor.matmul_mx(
                    out=acc[:, cols], lhsT=wt[t][:].bitcast(FP8X4), lhsT_scale=wst[t][:],
                    rhs=gw[:, cols].bitcast(FP4X4), rhs_scale=gs[:, cols], start=True, stop=True,
                )
            a = tl(f"a{t}", J, F32)
            top = tl(f"top{t}", 1, F32)
            nb = tl(f"nb{t}", 1, F32)
            nc.vector.tensor_scalar(out=a[:], in0=acc[:], scalar1=1.0, scalar2=None, op0=ALU.mult, op1=ALU.max, accum_out=top[:])
            if t == 0:
                nc.scalar.activation(out=nb[:], in_=top[:], func=ACT.Identity, bias=lo_sb[:, t : t + 1], scale=-1.0)
            else:
                nc.vector.tensor_tensor(out=nb[:], in0=lo_sb[:, t : t + 1], in1=top[:], op=ALU.subtract)
            nc.scalar.activation(out=hid[:, t : PACK * O : PACK], in_=a[:].indirect(list2[:]), func=ACT.Exp, bias=nb[:])

        hw = tl("hw", O, U32)
        hs = tl("hs", O, U8)
        nc.vector.quantize_mx(out=hw[:].bitcast(FP8X4), scales=hs[:], in_=hid[:])

        for c in range(CHUNKS):
            acc2 = ps.tile([P, O], F32, name=f"pacc{c}")
            nc.tensor.matmul_mx(
                out=acc2[:], lhsT=bw[:, 2 * P * c : 2 * P * (c + 1)].bitcast(FP4X4), lhsT_scale=bs[:, P * c : P * (c + 1)],
                rhs=hw[:].bitcast(FP8X4), rhs_scale=hs[:], start=True, stop=True,
            )
            prod = tl(f"prod{c}", O, F32)
            nc.vector.tensor_copy(prod[:], acc2[:])
            nc.scalar.activation(out=pages[c][:].indirect(list3[:]), in_=prod[:], func=ACT.Copy, scale=so_sb[:, c : c + 1])
            nc.sync.dma_start(out[P * c : P * (c + 1), :], pages[c][:])
